import numpy as np
import ml_dtypes


def mxq(x, axis, fmt="e4m3"):
    dtype, down = {"e4m3": (ml_dtypes.float8_e4m3fn, 7), "e5m2": (ml_dtypes.float8_e5m2, 14)}[fmt]
    v = np.moveaxis(np.asarray(x, np.float32).astype(ml_dtypes.bfloat16).astype(np.float64), axis, -1)
    blocks = v.reshape(v.shape[:-1] + (-1, 32))
    amax = np.abs(blocks).max(-1, keepdims=True)
    byte = np.maximum(np.where(amax > 0, np.frexp(amax)[1] - 1 + 127, 0) - down, 1)
    scale = np.exp2(byte - 127.0)
    codes = (blocks / scale).astype(np.float32).astype(dtype).astype(np.float64)
    return np.moveaxis((codes * scale).reshape(v.shape), -1, axis)


WIDE = False


def mx_kscale(k):
    if not WIDE:
        return np.ones(k)
    levels = np.array([10, -10, 5, -5, 0])
    if k % 512:
        return np.exp2(np.random.permutation(np.resize(levels, k // 32))).repeat(32)
    a = np.empty((k // 512, 16))
    for p in range(k // 512):
        a[p, :8] = np.random.permutation(np.resize(levels, 8))
        for g in range(8):
            far = levels[np.abs(levels - a[p, g]) >= 10]
            a[p, g + 8] = far[np.random.randint(len(far))]
    return np.exp2(a.ravel()).repeat(32)


def f64(x):
    return np.asarray(x).astype(np.float64)


def striped(idx):
    return np.tile(idx.reshape(-1, 16).T, (8, 1)).astype(np.uint16)


def unstriped(offs):
    return offs[:16].T.reshape(-1).astype(np.int64)


def striped8(idx):
    return np.concatenate([x.reshape(-1, 16).T for x in idx]).astype(np.uint16)


def runs(offs, k):
    lists = np.stack([offs[16 * r : 16 * r + 16].T.reshape(-1) for r in range(8)]).astype(np.int64)
    return lists[np.arange(k) % 512 // 64]


def pack_weight(w):
    k, n = w.shape
    w = f64(np.asarray(w, np.float32).astype(ml_dtypes.bfloat16)).reshape(k // 32, 32, n)
    amax = np.abs(w).max(1)
    byte = np.clip(np.where(amax > 0, np.frexp(amax)[1] - 1 + 127 - 7, 1), 1, 254)
    scaled = (w * np.exp2(127.0 - byte)[:, None, :]).reshape(k, n).astype(np.float32)
    words = np.ascontiguousarray(scaled.reshape(k // 512, 128, 4, n).transpose(0, 1, 3, 2)).astype(ml_dtypes.float8_e4m3fn).view(np.uint8)
    return words, np.ascontiguousarray(byte.astype(np.uint8).reshape(k // 512, 16, n))


def unpack_weight(words, scales):
    g, p, n, _ = words.shape
    vals = np.ascontiguousarray(words).view(ml_dtypes.float8_e4m3fn).astype(np.float64) * np.repeat(np.exp2(scales.astype(np.float64) - 127.0), 8, axis=1)[..., None]
    return vals.transpose(0, 1, 3, 2).reshape(g * 512, n)


E2M1 = np.array([0.0, 0.5, 1.0, 1.5, 2.0, 3.0, 4.0, 6.0, -0.0, -0.5, -1.0, -1.5, -2.0, -3.0, -4.0, -6.0])


def pack_fp4(w):
    k, n = w.shape
    w = f64(np.asarray(w, np.float32).astype(ml_dtypes.bfloat16)).reshape(k // 32, 32, n)
    amax = np.abs(w).max(1)
    mant, ex = np.frexp(amax / 6.0)
    byte = np.clip(np.where(amax > 0, np.where(mant > 0.5, ex, ex - 1) + 127, 1), 1, 254)
    scaled = (w * np.exp2(127.0 - byte)[:, None, :]).reshape(k, n).astype(np.float32)
    c = np.ascontiguousarray(scaled.reshape(k // 512, 128, 4, n).transpose(0, 1, 3, 2)).astype(ml_dtypes.float4_e2m1fn).view(np.uint8) & 0xF
    words = (c[..., 0::2] | (c[..., 1::2] << 4)).reshape(k // 512, 128, 2 * n)
    return np.ascontiguousarray(words), np.ascontiguousarray(byte.astype(np.uint8).reshape(k // 512, 16, n))


def unpack_fp4(words, scales):
    g, _, n = scales.shape
    words = np.ascontiguousarray(words).reshape(g, 128, n, 2)
    nib = np.empty((g, 128, n, 4), np.uint8)
    nib[..., 0::2] = words & 0xF
    nib[..., 1::2] = words >> 4
    vals = E2M1[nib] * np.repeat(np.exp2(scales.astype(np.float64) - 127.0), 8, axis=1)[..., None]
    return vals.transpose(0, 1, 3, 2).reshape(g * 512, n)


def sigmoid(v):
    return 1.0 / (1.0 + np.exp(-np.maximum(v, -700.0)))

def planes(y):
    n, m = y.shape
    v = y.astype(np.float32).astype(ml_dtypes.bfloat16).astype(np.float64).reshape(n // 32, 32, m)
    top = np.abs(v).max(1)
    byte = np.clip(np.where(top > 0, np.frexp(top)[1] - 1 + 127 - 7, 1), 1, 254)
    codes = (v * np.exp2(127.0 - byte)[:, None, :]).reshape(n, m).astype(np.float32).astype(ml_dtypes.float8_e4m3fn).view(np.uint8)
    words = codes.reshape(n // 512, 128, 4, m).transpose(0, 1, 3, 2)
    return np.ascontiguousarray(words), np.ascontiguousarray(byte.astype(np.uint8).reshape(n // 512, 16, m))


K, T, S, N, G, H = 512, 1024, 512, 512, 2048, 512


def setup_inputs():
    n = np.random.standard_normal
    s = mx_kscale(K)[:, None]
    u = mx_kscale(S)
    packed_xT = pack_weight(n((K, T)) * s)
    packed_dT = pack_weight(n((K, G)) / s)
    packed_w1 = pack_fp4(n((H, N)) / np.sqrt(H) / u[:, None])
    return {
        "x_words": packed_xT[0],
        "x_scales": packed_xT[1],
        "d_words": packed_dT[0],
        "d_scales": packed_dT[1],
        "gn": (np.random.uniform(0.5, 1.5, (H, 1)) * u[:, None]).astype(np.float32),
        "w1_words": packed_w1[0],
        "w1_scales": packed_w1[1],
        "offs": striped(np.random.permutation(T)[:S]),
        "k1": striped8(np.random.randint(0, G, (8, H))),
        "two": striped(np.random.permutation(T)[:S]),
        "k2": striped8(np.random.randint(0, G, (8, H))),
        "n1": striped8(np.stack([np.random.permutation(S) for _ in range(8)])),
        "n2": striped8(np.stack([np.random.permutation(S) for _ in range(8)])),
        "n3": striped(np.random.randint(0, S, G)),
    }


def reference(x_words, x_scales, d_words, d_scales, gn, w1_words, w1_scales, offs, k1, two, k2, n1, n2, n3):
    d_k1 = unpack_weight(d_words, d_scales)[np.arange(K)[:, None], runs(k1, K)]
    xq = unpack_weight(x_words, x_scales)[:, unstriped(offs)]
    a = 0.0625 * (d_k1.T @ xq)
    d_k2 = unpack_weight(d_words, d_scales)[np.arange(K)[:, None], runs(k2, K)]
    x_two = unpack_weight(x_words, x_scales)[:, unstriped(two)]
    b = 0.0625 * (d_k2.T @ x_two)
    z = f64(gn) * (a * (sigmoid(b[np.arange(H)[:, None], runs(n2, H)])) - (0.5 * (a[np.arange(H)[:, None], runs(n1, H)])))
    h = unpack_fp4(w1_words, w1_scales).T @ mxq(z, 0, "e4m3")
    mb = h[:, unstriped(n3)]
    sq = (mb) ** 2
    qs = sq.reshape(N, S, 4).sum(axis=2)
    out_0 = h / np.sqrt(qs + 0.5)
    return (out_0,) + planes(out_0)

@@ -1,0 +1,241 @@
+from contextlib import ExitStack
+
+import concourse.mybir as mybir
+
+K, T, S, N, G, H = 512, 1024, 512, 512, 2048, 512
+FLOPS = 3 * 2 * 512 * 512 * 512
+
+F32 = mybir.dt.float32
+BF16 = mybir.dt.bfloat16
+I32 = mybir.dt.int32
+U32 = mybir.dt.uint32
+U16 = mybir.dt.uint16
+U8 = mybir.dt.uint8
+FP8X4 = mybir.dt.float8_e4m3fn_x4
+FP4X4 = mybir.dt.float4_e2m1fn_x4
+ALU = mybir.AluOpType
+ACT = mybir.ActivationFunctionType
+
+P = 128
+PACK = 4
+HALF = S // 2
+CHUNK = 128
+MEMBERS = 4
+SPARE = 16
+
+
+def tile_picked_twpqgatebgvar_none_po_kernel(
+    tc, x_words, x_scales, d_words, d_scales, gn, w1_words, w1_scales, offs, k1, two, k2, n1, n2, n3, out_0, out_1, out_2
+):
+    nc = tc.nc
+    with ExitStack() as ctx:
+        keep = ctx.enter_context(tc.tile_pool(name="keep", bufs=1))
+        psum = ctx.enter_context(tc.psum_pool(name="psum", bufs=1))
+
+        def load_list(name, dram):
+            t = keep.tile(list(dram.shape), U16, name=name)
+            nc.sync.dma_start(t[:], dram)
+            return t
+
+        def zeroed_bytes(name, width, engine):
+            t = keep.tile([P, width], U8, name=name, align_bytes=64)
+            engine.memset(t[:].bitcast(I32), 0)
+            return t
+
+        def load_scale_rows(t, dram, queue):
+            for q in range(4):
+                queue.dma_start(t[32 * q : 32 * q + 4, :].bitcast(I32), dram[0, 4 * q : 4 * q + 4, :].bitcast(I32))
+
+        def load_block_scales(name, dram, width):
+            t = keep.tile([P, width], U8, name=name)
+            rows = dram[0].bitcast(I32).unsqueeze(1).to_broadcast([16, 8, width // 4])
+            nc.sync.dma_start(t[:].bitcast(I32), rows)
+            return t
+
+        def place_scale_rows(plane, picked):
+            for r in range(4):
+                nc.sync.dma_start(plane[r:P:32, :].bitcast(I32), picked[8 * r : P : 32, :].bitcast(I32))
+
+        k1_t = load_list("k1_t", k1)
+        d_sc = load_block_scales("d_sc", d_scales, G)
+        k2_t = load_list("k2_t", k2)
+        offs_t = load_list("offs_t", offs)
+        x_sc = load_block_scales("x_sc", x_scales, T)
+        two_t = load_list("two_t", two)
+        x_w = keep.tile([P, T], I32, name="x_w")
+        nc.sync.dma_start(x_w[:], x_words[0].rearrange("p c r -> p (c r)").bitcast(I32))
+        d_w = keep.tile([P, G], I32, name="d_w")
+        nc.sync.dma_start(d_w[:], d_words[0].rearrange("p c r -> p (c r)").bitcast(I32))
+        n1_t = load_list("n1_t", n1)
+        n2_t = load_list("n2_t", n2)
+        n3_t = load_list("n3_t", n3)
+        w_w = keep.tile([P, 2 * N], U8, name="w_w")
+        nc.sync.dma_start(w_w[:].bitcast(I32), w1_words[0].bitcast(I32))
+
+        w_sc = zeroed_bytes("w_sc", N, nc.gpsimd)
+        gain = keep.tile([P, PACK], F32, name="gain")
+        nc.sync.dma_start(gain[:], gn.rearrange("(p t) o -> p (t o)", t=PACK))
+        load_scale_rows(w_sc, w1_scales, nc.sync)
+        d_plane = zeroed_bytes("d_plane", 2 * H, nc.vector)
+        x_plane = zeroed_bytes("x_plane", 2 * S, nc.vector)
+
+        squares = [keep.tile([P, S + SPARE], F32, name=f"squares{t}") for t in range(PACK)]
+        for t in range(PACK):
+            nc.vector.memset(squares[t][:, S:], 0.0)
+
+        d_b = keep.tile([P, 2, H], U8, name="d_b")
+        for u, lst in enumerate((k1_t, k2_t)):
+            nc.vector.tensor_copy(d_b[:, u, :], d_sc[:].indirect(lst[:]))
+        d_bd = keep.tile([P, 2 * H], U8, name="d_bd")
+        nc.vector.tensor_copy(
+            d_bd[:].rearrange("p (u t m) -> p u m t", u=2, t=PACK), d_b[:].rearrange("p u (m t) -> p u m t", t=PACK)
+        )
+        place_scale_rows(d_plane, d_bd)
+        x_b = keep.tile([P, 2 * S], U8, name="x_b")
+        for u, lst in enumerate((offs_t, two_t)):
+            nc.vector.tensor_copy(x_b[:, S * u : S * (u + 1)], x_sc[:].indirect(lst[:]))
+        place_scale_rows(x_plane, x_b)
+
+        gain16 = keep.tile([P, PACK], F32, name="gain16")
+        nc.scalar.activation(gain16[:], gain[:], ACT.Copy, scale=0.0625)
+
+        def coded_product(u, tokens, codes):
+            xw = keep.tile([P, S], U32, name=f"xw{u}", align_bytes=64)
+            nc.vector.tensor_copy(xw[:], x_w[:].bitcast(U32).indirect(tokens[:]))
+            dw = keep.tile([P, H], U32, name=f"dw{u}", tag=f"dw{u}", align_bytes=64)
+            nc.vector.tensor_copy(dw[:], d_w[:].bitcast(U32).indirect(codes[:]))
+            dwd = keep.tile([P, H], U32, name=f"dwd{u}", align_bytes=64)
+            nc.vector.tensor_copy(
+                dwd[:].rearrange("p (t m) -> p m t", t=PACK), dw[:].rearrange("p (m t) -> p m t", t=PACK)
+            )
+            banks = []
+            for t in range(PACK):
+                bank = psum.tile([P, S], F32, name=f"bank{u}{t}", tag=f"bank{u}{t}")
+                nc.tensor.matmul_mx(
+                    out=bank[:],
+                    lhsT=dwd[:, P * t : P * (t + 1)].bitcast(FP8X4),
+                    lhsT_scale=d_plane[:, H * u + P * t : H * u + P * (t + 1)],
+                    rhs=xw[:].bitcast(FP8X4),
+                    rhs_scale=x_plane[:, S * u : S * (u + 1)],
+                    start=True,
+                    stop=True,
+                )
+                banks.append(bank)
+            return banks
+
+        a_banks = coded_product(0, offs_t, k1_t)
+        ga = [keep.tile([P, S], F32, name=f"ga{t}") for t in range(PACK)]
+        for t in range(PACK):
+            nc.scalar.activation(ga[t][:], a_banks[t][:], ACT.Copy, scale=gain16[:, t : t + 1])
+
+        b_banks = coded_product(1, two_t, k2_t)
+
+        w_wd = keep.tile([P, 2 * N], U8, name="w_wd", align_bytes=64)
+        nc.scalar.copy(
+            w_wd[:].bitcast(U16).rearrange("p (t m) -> p t m", t=PACK),
+            w_w[:].bitcast(U16).rearrange("p (m t) -> p t m", t=PACK),
+        )
+        w_sd = keep.tile([P, N], U8, name="w_sd", tag="dw1", align_bytes=64)
+        nc.vector.tensor_copy(
+            w_sd[:].rearrange("p (t m) -> p m t", t=PACK), w_sc[:].rearrange("p (m t) -> p m t", t=PACK)
+        )
+
+        half_ga = [keep.tile([P, PACK, HALF], F32, name=f"half_ga{v}") for v in range(2)]
+        gated = [keep.tile([P, PACK, HALF], F32, name=f"gated{v}") for v in range(2)]
+        gate = [keep.tile([P, S], F32, name=f"gate{t}") for t in range(PACK)]
+
+        def fetch_half_ga(v):
+            for t in range(PACK):
+                nc.scalar.activation(
+                    half_ga[v][:, t, :], ga[t][:].indirect(n1_t[:, 16 * v : 16 * (v + 1)]), ACT.Copy, scale=0.5
+                )
+
+        fetch_half_ga(0)
+        for t in range(PACK):
+            nc.scalar.activation(gate[t][:], b_banks[t][:], ACT.Sigmoid, scale=0.0625)
+        fetch_half_ga(1)
+
+        h_banks = {}
+        for v in range(2):
+            cols = slice(HALF * v, HALF * (v + 1))
+            for t in range(PACK):
+                nc.vector.tensor_tensor(
+                    gated[v][:, t, :], gate[t][:].indirect(n2_t[:, 16 * v : 16 * (v + 1)]), ga[t][:, cols], ALU.mult
+                )
+            zb = keep.tile([P, HALF * PACK], BF16, name=f"zb{v}", align_bytes=64)
+            nc.vector.tensor_tensor(
+                zb[:].rearrange("p (c i t) -> p c t i", i=4, t=PACK),
+                gated[v][:].rearrange("p t (c i) -> p c t i", i=4),
+                half_ga[v][:].rearrange("p t (c i) -> p c t i", i=4),
+                ALU.subtract,
+            )
+            zw = keep.tile([P, HALF], U32, name=f"zw{v}", align_bytes=64)
+            zs = keep.tile([P, HALF], U8, name=f"zs{v}", align_bytes=64)
+            nc.vector.quantize_mx(out=zw[:].bitcast(FP8X4), scales=zs[:], in_=zb[:])
+            for t in range(PACK):
+                bank = psum.tile([P, S], F32, name=f"h{v}{t}", tag=f"bank{v}{t}")
+                nc.tensor.matmul_mx(
+                    out=bank[:, :HALF],
+                    lhsT=w_wd[:, 2 * P * t : 2 * P * (t + 1)].bitcast(FP4X4),
+                    lhsT_scale=w_sd[:, P * t : P * (t + 1)],
+                    rhs=zw[:].bitcast(FP8X4),
+                    rhs_scale=zs[:],
+                    start=True,
+                    stop=True,
+                )
+                h_banks[v, t] = bank
+                nc.scalar.activation(squares[t][:, cols], bank[:, :HALF], ACT.Square)
+
+        out_rows = out_0.rearrange("(p t) j -> p t j", t=PACK)
+        out_words = out_1[0].rearrange("p c r -> p (c r)").bitcast(I32)
+        y_w = keep.tile([P, S], U32, name="y_w", align_bytes=64)
+        y_s = keep.tile([P, S], U8, name="y_s", align_bytes=64)
+        width = CHUNK * MEMBERS
+        sums = {}
+        roots = {}
+
+        def fetch(c):
+            fetched = keep.tile([P, PACK, width], F32, name=f"fetched{c}")
+            entries = n3_t[:, width // 16 * c : width // 16 * (c + 1)]
+            for t in range(PACK):
+                if t == 0:
+                    nc.vector.tensor_copy(fetched[:, t, :], squares[t][:].indirect(entries))
+                else:
+                    nc.scalar.activation(fetched[:, t, :], squares[t][:].indirect(entries), ACT.Copy)
+            return fetched
+
+        def add_up(c, fetched):
+            quads = fetched[:].rearrange("p t (j e) -> p (t j) e", e=MEMBERS)
+            pairs = keep.tile([P, PACK * CHUNK, 2], F32, name=f"pairs{c}")
+            nc.vector.tensor_tensor(pairs[:], quads[:, :, 0:2], quads[:, :, 2:4], ALU.add)
+            total = keep.tile([P, PACK * CHUNK], F32, name=f"total{c}")
+            nc.vector.scalar_tensor_tensor(total[:], pairs[:, :, 0], 0.5, pairs[:, :, 1], ALU.add, ALU.add)
+            root = keep.tile([P, PACK, CHUNK], F32, name=f"root{c}")
+            nc.scalar.activation(root[:].rearrange("p t j -> p (t j)"), total[:], ACT.Abs_reciprocal_sqrt)
+            return root
+
+        def finish(c, root):
+            v, at = divmod(CHUNK * c, HALF)
+            cols = slice(CHUNK * c, CHUNK * (c + 1))
+            y = keep.tile([P, PACK, CHUNK], F32, name=f"y{c}")
+            for t in range(PACK):
+                nc.vector.tensor_tensor(y[:, t, :], h_banks[v, t][:, at : at + CHUNK], root[:, t, :], ALU.mult)
+            nc.sync.dma_start(out_rows[:, :, cols], y[:])
+            yb = keep.tile([P, CHUNK * PACK], BF16, name=f"yb{c}", align_bytes=64)
+            nc.vector.tensor_copy(
+                yb[:].rearrange("p (c i t) -> p c t i", i=4, t=PACK), y[:].rearrange("p t (c i) -> p c t i", i=4)
+            )
+            nc.vector.quantize_mx(out=y_w[:, cols].bitcast(FP8X4), scales=y_s[:, cols], in_=yb[:])
+            nc.sync.dma_start(out_words[:, cols], y_w[:, cols].bitcast(I32))
+
+        chunks = S // CHUNK
+        for c in range(chunks + 2):
+            if c < chunks:
+                sums[c] = fetch(c)
+            if 1 <= c <= chunks:
+                roots[c - 1] = add_up(c - 1, sums[c - 1])
+            if c >= 2:
+                finish(c - 2, roots[c - 2])
+        for q in range(4):
+            queue = nc.sync if q % 2 else nc.scalar
+            queue.dma_start(out_2[0, 4 * q : 4 * q + 4, :].bitcast(I32), y_s[32 * q : 32 * q + 4, :].bitcast(I32))

@@ -19,7 +19,9 @@ ACT = mybir.ActivationFunctionType
 P = 128
 PACK = 4
 HALF = S // 2
-CHUNK = 128
+CHUNKS = (128, 128, 128, 64, 64,)
+PIECES = (256, 128, 128,)
+EARLY = 8
 MEMBERS = 4
 SPARE = 16
 
@@ -56,57 +58,58 @@ def tile_picked_twpqgatebgvar_none_po_kernel(
             for r in range(4):
                 nc.sync.dma_start(plane[r:P:32, :].bitcast(I32), picked[8 * r : P : 32, :].bitcast(I32))
 
-        k1_t = load_list("k1_t", k1)
-        d_sc = load_block_scales("d_sc", d_scales, G)
-        k2_t = load_list("k2_t", k2)
         offs_t = load_list("offs_t", offs)
         x_sc = load_block_scales("x_sc", x_scales, T)
-        two_t = load_list("two_t", two)
-        x_w = keep.tile([P, T], I32, name="x_w")
+        k1_t = load_list("k1_t", k1)
+        d_sc = load_block_scales("d_sc", d_scales, G)
+        x_w = keep.tile([P, T], I32, name="x_w", tag="x_w")
         nc.sync.dma_start(x_w[:], x_words[0].rearrange("p c r -> p (c r)").bitcast(I32))
         d_w = keep.tile([P, G], I32, name="d_w")
         nc.sync.dma_start(d_w[:], d_words[0].rearrange("p c r -> p (c r)").bitcast(I32))
+        k2_t = load_list("k2_t", k2)
+        two_t = load_list("two_t", two)
         n1_t = load_list("n1_t", n1)
         n2_t = load_list("n2_t", n2)
         n3_t = load_list("n3_t", n3)
-        w_w = keep.tile([P, 2 * N], U8, name="w_w")
-        nc.sync.dma_start(w_w[:].bitcast(I32), w1_words[0].bitcast(I32))
 
-        w_sc = zeroed_bytes("w_sc", N, nc.gpsimd)
         gain = keep.tile([P, PACK], F32, name="gain")
-        nc.sync.dma_start(gain[:], gn.rearrange("(p t) o -> p (t o)", t=PACK))
-        load_scale_rows(w_sc, w1_scales, nc.sync)
-        d_plane = zeroed_bytes("d_plane", 2 * H, nc.vector)
-        x_plane = zeroed_bytes("x_plane", 2 * S, nc.vector)
+        nc.gpsimd.dma_start(gain[:], gn.rearrange("(p t) o -> p (t o)", t=PACK))
+        w_sc = zeroed_bytes("w_sc", N, nc.gpsimd)
+        load_scale_rows(w_sc, w1_scales, nc.gpsimd)
+        w_w = keep.tile([P, 2 * N], U8, name="w_w")
+        nc.gpsimd.dma_start(w_w[:].bitcast(I32), w1_words[0].bitcast(I32))
+        planes = [zeroed_bytes(f"plane{u}", H + S, nc.vector) for u in range(2)]
 
         squares = [keep.tile([P, S + SPARE], F32, name=f"squares{t}") for t in range(PACK)]
         for t in range(PACK):
             nc.vector.memset(squares[t][:, S:], 0.0)
 
-        d_b = keep.tile([P, 2, H], U8, name="d_b")
-        for u, lst in enumerate((k1_t, k2_t)):
-            nc.vector.tensor_copy(d_b[:, u, :], d_sc[:].indirect(lst[:]))
-        d_bd = keep.tile([P, 2 * H], U8, name="d_bd")
-        nc.vector.tensor_copy(
-            d_bd[:].rearrange("p (u t m) -> p u m t", u=2, t=PACK), d_b[:].rearrange("p u (m t) -> p u m t", t=PACK)
-        )
-        place_scale_rows(d_plane, d_bd)
-        x_b = keep.tile([P, 2 * S], U8, name="x_b")
-        for u, lst in enumerate((offs_t, two_t)):
-            nc.vector.tensor_copy(x_b[:, S * u : S * (u + 1)], x_sc[:].indirect(lst[:]))
-        place_scale_rows(x_plane, x_b)
-
         gain16 = keep.tile([P, PACK], F32, name="gain16")
         nc.scalar.activation(gain16[:], gain[:], ACT.Copy, scale=0.0625)
 
         def coded_product(u, tokens, codes):
-            xw = keep.tile([P, S], U32, name=f"xw{u}", align_bytes=64)
-            nc.vector.tensor_copy(xw[:], x_w[:].bitcast(U32).indirect(tokens[:]))
-            dw = keep.tile([P, H], U32, name=f"dw{u}", tag=f"dw{u}", align_bytes=64)
-            nc.vector.tensor_copy(dw[:], d_w[:].bitcast(U32).indirect(codes[:]))
+            picked = keep.tile([P, H + S], U8, name=f"picked{u}", tag="picked_bytes" if u == 0 else "picked_words", align_bytes=64)
+            nc.vector.tensor_copy(picked[:, H:], x_sc[:].indirect(tokens[:]))
+            nc.vector.tensor_copy(picked[:, :H], d_sc[:].indirect(codes[:]))
+            dealt = keep.tile([P, H + S], U8, name=f"dealt{u}", tag=f"dealt{u}", align_bytes=64)
+            nc.vector.tensor_copy(dealt[:, H:].bitcast(I32), picked[:, H:].bitcast(I32))
+            nc.vector.tensor_copy(
+                dealt[:, :H].rearrange("p (t m) -> p m t", t=PACK), picked[:, :H].rearrange("p (m t) -> p m t", t=PACK)
+            )
+            place_scale_rows(planes[u], dealt)
+            if u == 0:
+                xw = keep.tile([P, S], U32, name="xw0", align_bytes=64)[:]
+                dw = keep.tile([P, H], U32, name="dw0", tag="picked_words", align_bytes=64)[:]
+                nc.vector.tensor_copy(xw, x_w[:].bitcast(U32).indirect(tokens[:]))
+                nc.vector.tensor_copy(dw, d_w[:].bitcast(U32).indirect(codes[:]))
+            else:
+                both = keep.tile([P, H + S], U32, name="both", tag="picked_words", align_bytes=64)
+                dw, xw = both[:, :H], both[:, H:]
+                nc.vector.tensor_copy(dw, d_w[:].bitcast(U32).indirect(codes[:]))
+                nc.vector.tensor_copy(xw, x_w[:].bitcast(U32).indirect(tokens[:]))
             dwd = keep.tile([P, H], U32, name=f"dwd{u}", align_bytes=64)
             nc.vector.tensor_copy(
-                dwd[:].rearrange("p (t m) -> p m t", t=PACK), dw[:].rearrange("p (m t) -> p m t", t=PACK)
+                dwd[:].rearrange("p (t m) -> p m t", t=PACK), dw.rearrange("p (m t) -> p m t", t=PACK)
             )
             banks = []
             for t in range(PACK):
@@ -114,9 +117,9 @@ def tile_picked_twpqgatebgvar_none_po_kernel(
                 nc.tensor.matmul_mx(
                     out=bank[:],
                     lhsT=dwd[:, P * t : P * (t + 1)].bitcast(FP8X4),
-                    lhsT_scale=d_plane[:, H * u + P * t : H * u + P * (t + 1)],
-                    rhs=xw[:].bitcast(FP8X4),
-                    rhs_scale=x_plane[:, S * u : S * (u + 1)],
+                    lhsT_scale=planes[u][:, P * t : P * (t + 1)],
+                    rhs=xw.bitcast(FP8X4),
+                    rhs_scale=planes[u][:, H:],
                     start=True,
                     stop=True,
                 )
@@ -130,112 +133,139 @@ def tile_picked_twpqgatebgvar_none_po_kernel(
 
         b_banks = coded_product(1, two_t, k2_t)
 
-        w_wd = keep.tile([P, 2 * N], U8, name="w_wd", align_bytes=64)
-        nc.scalar.copy(
-            w_wd[:].bitcast(U16).rearrange("p (t m) -> p t m", t=PACK),
-            w_w[:].bitcast(U16).rearrange("p (m t) -> p t m", t=PACK),
-        )
-        w_sd = keep.tile([P, N], U8, name="w_sd", tag="dw1", align_bytes=64)
+        w_sd = keep.tile([P, N], U8, name="w_sd", tag="dealt1", align_bytes=64)
         nc.vector.tensor_copy(
             w_sd[:].rearrange("p (t m) -> p m t", t=PACK), w_sc[:].rearrange("p (m t) -> p m t", t=PACK)
         )
 
-        half_ga = [keep.tile([P, PACK, HALF], F32, name=f"half_ga{v}") for v in range(2)]
-        gated = [keep.tile([P, PACK, HALF], F32, name=f"gated{v}") for v in range(2)]
+        pieces = []
+        for width in PIECES:
+            first = sum(PIECES[: len(pieces)])
+            pieces.append(slice(first, first + width))
+        last = len(PIECES) - 1
+        half_ga = [
+            keep.tile([P, PACK, w], F32, name=f"half_ga{v}", tag="x_w" if v == last else f"half_ga{v}")
+            for v, w in enumerate(PIECES)
+        ]
+        gated = {}
         gate = [keep.tile([P, S], F32, name=f"gate{t}") for t in range(PACK)]
 
-        def fetch_half_ga(v):
-            for t in range(PACK):
-                nc.scalar.activation(
-                    half_ga[v][:, t, :], ga[t][:].indirect(n1_t[:, 16 * v : 16 * (v + 1)]), ACT.Copy, scale=0.5
-                )
+        def entries(lst, cols):
+            return lst[:, cols.start // 16 : cols.stop // 16]
 
-        fetch_half_ga(0)
+        jobs = [(v, t) for v in range(len(PIECES)) for t in range(PACK)]
+
+        def fetch_half_ga(some):
+            for v, t in some:
+                looked_up = ga[t][:].indirect(entries(n1_t, pieces[v]))
+                if v == last and t < 4:
+                    nc.vector.tensor_scalar(half_ga[v][:, t, :], looked_up, 0.5, 0.0, ALU.mult, ALU.add)
+                else:
+                    nc.scalar.activation(half_ga[v][:, t, :], looked_up, ACT.Copy, scale=0.5)
+
+        fetch_half_ga(jobs[:EARLY])
         for t in range(PACK):
             nc.scalar.activation(gate[t][:], b_banks[t][:], ACT.Sigmoid, scale=0.0625)
-        fetch_half_ga(1)
+        fetch_half_ga(jobs[EARLY:])
 
+        w_wd = keep.tile([P, 2 * N], U8, name="w_wd", align_bytes=64)
         h_banks = {}
-        for v in range(2):
-            cols = slice(HALF * v, HALF * (v + 1))
+        def mix(v, t):
+            if t == 0:
+                gated[v] = keep.tile([P, PACK, PIECES[v]], F32, name=f"gated{v}", tag="gated", bufs=2)
+            looked_up = gate[t][:].indirect(entries(n2_t, pieces[v]))
+            if v >= 1:
+                fetched_gate = keep.tile([P, PIECES[v]], F32, name=f"fetched_gate{v}{t}")
+                nc.scalar.activation(fetched_gate[:], looked_up, ACT.Copy)
+                looked_up = fetched_gate[:]
+            nc.vector.tensor_tensor(gated[v][:, t, :], looked_up, ga[t][:, pieces[v]], ALU.mult)
+
+        nc.scalar.copy(
+            w_wd[:].bitcast(U16).rearrange("p (t m) -> p t m", t=PACK),
+            w_w[:].bitcast(U16).rearrange("p (m t) -> p t m", t=PACK),
+        )
+
+        for v, cols in enumerate(pieces):
+            width = PIECES[v]
             for t in range(PACK):
-                nc.vector.tensor_tensor(
-                    gated[v][:, t, :], gate[t][:].indirect(n2_t[:, 16 * v : 16 * (v + 1)]), ga[t][:, cols], ALU.mult
-                )
-            zb = keep.tile([P, HALF * PACK], BF16, name=f"zb{v}", align_bytes=64)
+                mix(v, t)
+            zb = keep.tile([P, width * PACK], BF16, name=f"zb{v}", tag="zb", bufs=2, align_bytes=64)
             nc.vector.tensor_tensor(
                 zb[:].rearrange("p (c i t) -> p c t i", i=4, t=PACK),
                 gated[v][:].rearrange("p t (c i) -> p c t i", i=4),
                 half_ga[v][:].rearrange("p t (c i) -> p c t i", i=4),
                 ALU.subtract,
             )
-            zw = keep.tile([P, HALF], U32, name=f"zw{v}", align_bytes=64)
-            zs = keep.tile([P, HALF], U8, name=f"zs{v}", align_bytes=64)
+            zw = keep.tile([P, width], U32, name=f"zw{v}", align_bytes=64)
+            zs = keep.tile([P, width], U8, name=f"zs{v}", align_bytes=64)
             nc.vector.quantize_mx(out=zw[:].bitcast(FP8X4), scales=zs[:], in_=zb[:])
-            for t in range(PACK):
-                bank = psum.tile([P, S], F32, name=f"h{v}{t}", tag=f"bank{v}{t}")
-                nc.tensor.matmul_mx(
-                    out=bank[:, :HALF],
-                    lhsT=w_wd[:, 2 * P * t : 2 * P * (t + 1)].bitcast(FP4X4),
-                    lhsT_scale=w_sd[:, P * t : P * (t + 1)],
-                    rhs=zw[:].bitcast(FP8X4),
-                    rhs_scale=zs[:],
-                    start=True,
-                    stop=True,
-                )
-                h_banks[v, t] = bank
-                nc.scalar.activation(squares[t][:, cols], bank[:, :HALF], ACT.Square)
+            for at in range(0, width, P):
+                side = (cols.start + at) // P
+                h_banks[side] = psum.tile([P, PACK, P], F32, name=f"h{side}", tag=f"bank0{side}")
+                for t in range(PACK):
+                    nc.tensor.matmul_mx(
+                        out=h_banks[side][:, t, :],
+                        lhsT=w_wd[:, 2 * P * t : 2 * P * (t + 1)].bitcast(FP4X4),
+                        lhsT_scale=w_sd[:, P * t : P * (t + 1)],
+                        rhs=zw[:, at : at + P].bitcast(FP8X4),
+                        rhs_scale=zs[:, at : at + P],
+                        start=True,
+                        stop=True,
+                    )
+                for t in range(PACK):
+                    nc.scalar.activation(squares[t][:, P * side : P * (side + 1)], h_banks[side][:, t, :], ACT.Square)
 
         out_rows = out_0.rearrange("(p t) j -> p t j", t=PACK)
         out_words = out_1[0].rearrange("p c r -> p (c r)").bitcast(I32)
         y_w = keep.tile([P, S], U32, name="y_w", align_bytes=64)
         y_s = keep.tile([P, S], U8, name="y_s", align_bytes=64)
-        width = CHUNK * MEMBERS
-        sums = {}
+        chunks = []
+        for width in CHUNKS:
+            first = sum(CHUNKS[: len(chunks)])
+            chunks.append(slice(first, first + width))
+        fetched = {}
         roots = {}
 
         def fetch(c):
-            fetched = keep.tile([P, PACK, width], F32, name=f"fetched{c}")
-            entries = n3_t[:, width // 16 * c : width // 16 * (c + 1)]
+            width = CHUNKS[c] * MEMBERS
+            fetched[c] = keep.tile([P, PACK, width], F32, name=f"fetched{c}", tag="fetched", bufs=3)
+            members = entries(n3_t, slice(chunks[c].start * MEMBERS, chunks[c].stop * MEMBERS))
             for t in range(PACK):
-                if t == 0:
-                    nc.vector.tensor_copy(fetched[:, t, :], squares[t][:].indirect(entries))
+                if t < (2, 2, 1, 1, 0)[c]:
+                    nc.vector.tensor_copy(fetched[c][:, t, :], squares[t][:].indirect(members))
                 else:
-                    nc.scalar.activation(fetched[:, t, :], squares[t][:].indirect(entries), ACT.Copy)
-            return fetched
+                    nc.scalar.activation(fetched[c][:, t, :], squares[t][:].indirect(members), ACT.Copy)
 
-        def add_up(c, fetched):
-            quads = fetched[:].rearrange("p t (j e) -> p (t j) e", e=MEMBERS)
-            pairs = keep.tile([P, PACK * CHUNK, 2], F32, name=f"pairs{c}")
+        def add_up(c):
+            width = CHUNKS[c]
+            quads = fetched[c][:].rearrange("p t (j e) -> p (t j) e", e=MEMBERS)
+            pairs = keep.tile([P, PACK * width, 2], F32, name=f"pairs{c}")
             nc.vector.tensor_tensor(pairs[:], quads[:, :, 0:2], quads[:, :, 2:4], ALU.add)
-            total = keep.tile([P, PACK * CHUNK], F32, name=f"total{c}")
-            nc.vector.scalar_tensor_tensor(total[:], pairs[:, :, 0], 0.5, pairs[:, :, 1], ALU.add, ALU.add)
-            root = keep.tile([P, PACK, CHUNK], F32, name=f"root{c}")
-            nc.scalar.activation(root[:].rearrange("p t j -> p (t j)"), total[:], ACT.Abs_reciprocal_sqrt)
-            return root
+            total = fetched[c][:, 0, :]
+            nc.vector.scalar_tensor_tensor(total, pairs[:, :, 0], 0.5, pairs[:, :, 1], ALU.add, ALU.add)
+            roots[c] = keep.tile([P, PACK, width], F32, name=f"root{c}")
+            nc.scalar.activation(roots[c][:].rearrange("p t j -> p (t j)"), total, ACT.Abs_reciprocal_sqrt)
 
-        def finish(c, root):
-            v, at = divmod(CHUNK * c, HALF)
-            cols = slice(CHUNK * c, CHUNK * (c + 1))
-            y = keep.tile([P, PACK, CHUNK], F32, name=f"y{c}")
-            for t in range(PACK):
-                nc.vector.tensor_tensor(y[:, t, :], h_banks[v, t][:, at : at + CHUNK], root[:, t, :], ALU.mult)
+        def finish(c):
+            width, cols = CHUNKS[c], chunks[c]
+            side, at = divmod(cols.start, P)
+            y = keep.tile([P, PACK, width], F32, name=f"y{c}")
+            nc.vector.tensor_tensor(y[:], h_banks[side][:, :, at : at + width], roots[c][:], ALU.mult)
             nc.sync.dma_start(out_rows[:, :, cols], y[:])
-            yb = keep.tile([P, CHUNK * PACK], BF16, name=f"yb{c}", align_bytes=64)
+            yb = keep.tile([P, width * PACK], BF16, name=f"yb{c}", align_bytes=64)
             nc.vector.tensor_copy(
                 yb[:].rearrange("p (c i t) -> p c t i", i=4, t=PACK), y[:].rearrange("p t (c i) -> p c t i", i=4)
             )
             nc.vector.quantize_mx(out=y_w[:, cols].bitcast(FP8X4), scales=y_s[:, cols], in_=yb[:])
             nc.sync.dma_start(out_words[:, cols], y_w[:, cols].bitcast(I32))
 
-        chunks = S // CHUNK
-        for c in range(chunks + 2):
-            if c < chunks:
-                sums[c] = fetch(c)
-            if 1 <= c <= chunks:
-                roots[c - 1] = add_up(c - 1, sums[c - 1])
+        for c in range(len(CHUNKS) + 2):
+            if 1 <= c <= len(CHUNKS):
+                add_up(c - 1)
             if c >= 2:
-                finish(c - 2, roots[c - 2])
+                finish(c - 2)
+            if c < len(CHUNKS):
+                fetch(c)
         for q in range(4):
             queue = nc.sync if q % 2 else nc.scalar
             queue.dma_start(out_2[0, 4 * q : 4 * q + 4, :].bitcast(I32), y_s[32 * q : 32 * q + 4, :].bitcast(I32))

@@ -83,6 +83,8 @@ def tile_picked_twpqgatebgvar_none_po_kernel(
         squares = [keep.tile([P, S + SPARE], F32, name=f"squares{t}") for t in range(PACK)]
         for t in range(PACK):
             nc.vector.memset(squares[t][:, S:], 0.0)
+        warm = keep.tile([P, 2], F32, name="warm")
+        nc.scalar.activation(warm[:, 0:1], gain[:, 0:1], ACT.Sigmoid)
 
         gain16 = keep.tile([P, PACK], F32, name="gain16")
         nc.scalar.activation(gain16[:], gain[:], ACT.Copy, scale=0.0625)
@@ -179,6 +181,7 @@ def tile_picked_twpqgatebgvar_none_po_kernel(
                 nc.scalar.activation(fetched_gate[:], looked_up, ACT.Copy)
                 looked_up = fetched_gate[:]
             nc.vector.tensor_tensor(gated[v][:, t, :], looked_up, ga[t][:, pieces[v]], ALU.mult)
+            return looked_up
 
         nc.scalar.copy(
             w_wd[:].bitcast(U16).rearrange("p (t m) -> p t m", t=PACK),
@@ -188,7 +191,9 @@ def tile_picked_twpqgatebgvar_none_po_kernel(
         for v, cols in enumerate(pieces):
             width = PIECES[v]
             for t in range(PACK):
-                mix(v, t)
+                newest = mix(v, t)
+            if v == last:
+                nc.scalar.activation(warm[:, 1:2], newest[:, 0:1], ACT.Abs_reciprocal_sqrt, bias=0.5)
             zb = keep.tile([P, width * PACK], BF16, name=f"zb{v}", tag="zb", bufs=2, align_bytes=64)
             nc.vector.tensor_tensor(
                 zb[:].rearrange("p (c i t) -> p c t i", i=4, t=PACK),

@@ -1,6 +1,7 @@
 from contextlib import ExitStack
 
 import concourse.mybir as mybir
+from concourse.masks import make_identity
 
 K, T, S, N, G, H = 512, 1024, 512, 512, 2048, 512
 FLOPS = 3 * 2 * 512 * 512 * 512
@@ -24,6 +25,7 @@ PIECES = (256, 128, 128,)
 EARLY = 8
 MEMBERS = 4
 SPARE = 16
+ON_TENSOR = (0, 1)
 
 
 def tile_picked_twpqgatebgvar_none_po_kernel(
@@ -64,10 +66,10 @@ def tile_picked_twpqgatebgvar_none_po_kernel(
         d_sc = load_block_scales("d_sc", d_scales, G)
         x_w = keep.tile([P, T], I32, name="x_w", tag="x_w")
         nc.sync.dma_start(x_w[:], x_words[0].rearrange("p c r -> p (c r)").bitcast(I32))
-        d_w = keep.tile([P, G], I32, name="d_w")
-        nc.sync.dma_start(d_w[:], d_words[0].rearrange("p c r -> p (c r)").bitcast(I32))
         k2_t = load_list("k2_t", k2)
         two_t = load_list("two_t", two)
+        d_w = keep.tile([P, G], I32, name="d_w")
+        nc.sync.dma_start(d_w[:], d_words[0].rearrange("p c r -> p (c r)").bitcast(I32))
         n1_t = load_list("n1_t", n1)
         n2_t = load_list("n2_t", n2)
         n3_t = load_list("n3_t", n3)
@@ -86,6 +88,8 @@ def tile_picked_twpqgatebgvar_none_po_kernel(
         warm = keep.tile([P, 2], F32, name="warm")
         nc.scalar.activation(warm[:, 0:1], gain[:, 0:1], ACT.Sigmoid)
 
+        ident = keep.tile([P, P], F32, name="ident")
+        make_identity(nc, ident[:])
         gain16 = keep.tile([P, PACK], F32, name="gain16")
         nc.scalar.activation(gain16[:], gain[:], ACT.Copy, scale=0.0625)
 
@@ -96,7 +100,7 @@ def tile_picked_twpqgatebgvar_none_po_kernel(
             dealt = keep.tile([P, H + S], U8, name=f"dealt{u}", tag=f"dealt{u}", align_bytes=64)
             nc.vector.tensor_copy(dealt[:, H:].bitcast(I32), picked[:, H:].bitcast(I32))
             nc.vector.tensor_copy(
-                dealt[:, :H].rearrange("p (t m) -> p m t", t=PACK), picked[:, :H].rearrange("p (m t) -> p m t", t=PACK)
+                dealt[:, :H].rearrange("p (t m) -> p t m", t=PACK), picked[:, :H].rearrange("p (m t) -> p t m", t=PACK)
             )
             place_scale_rows(planes[u], dealt)
             if u == 0:
@@ -111,7 +115,7 @@ def tile_picked_twpqgatebgvar_none_po_kernel(
                 nc.vector.tensor_copy(xw, x_w[:].bitcast(U32).indirect(tokens[:]))
             dwd = keep.tile([P, H], U32, name=f"dwd{u}", align_bytes=64)
             nc.vector.tensor_copy(
-                dwd[:].rearrange("p (t m) -> p m t", t=PACK), dw.rearrange("p (m t) -> p m t", t=PACK)
+                dwd[:].rearrange("p (t c i) -> p c t i", t=PACK, i=4), dw.rearrange("p (c i t) -> p c t i", t=PACK, i=4)
             )
             banks = []
             for t in range(PACK):
@@ -137,7 +141,7 @@ def tile_picked_twpqgatebgvar_none_po_kernel(
 
         w_sd = keep.tile([P, N], U8, name="w_sd", tag="dealt1", align_bytes=64)
         nc.vector.tensor_copy(
-            w_sd[:].rearrange("p (t m) -> p m t", t=PACK), w_sc[:].rearrange("p (m t) -> p m t", t=PACK)
+            w_sd[:].rearrange("p (t m) -> p t m", t=PACK), w_sc[:].rearrange("p (m t) -> p t m", t=PACK)
         )
 
         pieces = []
@@ -150,6 +154,7 @@ def tile_picked_twpqgatebgvar_none_po_kernel(
             for v, w in enumerate(PIECES)
         ]
         gated = {}
+        fetched_gate = {}
         gate = [keep.tile([P, S], F32, name=f"gate{t}") for t in range(PACK)]
 
         def entries(lst, cols):
@@ -172,14 +177,17 @@ def tile_picked_twpqgatebgvar_none_po_kernel(
 
         w_wd = keep.tile([P, 2 * N], U8, name="w_wd", align_bytes=64)
         h_banks = {}
+        h_kept = {}
         def mix(v, t):
             if t == 0:
                 gated[v] = keep.tile([P, PACK, PIECES[v]], F32, name=f"gated{v}", tag="gated", bufs=2)
             looked_up = gate[t][:].indirect(entries(n2_t, pieces[v]))
             if v >= 1:
-                fetched_gate = keep.tile([P, PIECES[v]], F32, name=f"fetched_gate{v}{t}")
-                nc.scalar.activation(fetched_gate[:], looked_up, ACT.Copy)
-                looked_up = fetched_gate[:]
+                if v == 1:
+                    rest = slice(PIECES[0], S)
+                    fetched_gate[t] = keep.tile([P, S - PIECES[0]], F32, name=f"fetched_gate{t}")
+                    nc.scalar.activation(fetched_gate[t][:], gate[t][:].indirect(entries(n2_t, rest)), ACT.Copy)
+                looked_up = fetched_gate[t][:, pieces[v].start - PIECES[0] : pieces[v].stop - PIECES[0]]
             nc.vector.tensor_tensor(gated[v][:, t, :], looked_up, ga[t][:, pieces[v]], ALU.mult)
             return looked_up
 
@@ -194,7 +202,7 @@ def tile_picked_twpqgatebgvar_none_po_kernel(
                 newest = mix(v, t)
             if v == last:
                 nc.scalar.activation(warm[:, 1:2], newest[:, 0:1], ACT.Abs_reciprocal_sqrt, bias=0.5)
-            zb = keep.tile([P, width * PACK], BF16, name=f"zb{v}", tag="zb", bufs=2, align_bytes=64)
+            zb = keep.tile([P, width * PACK], BF16, name=f"zb{v}", tag=f"zb{v}", align_bytes=64)
             nc.vector.tensor_tensor(
                 zb[:].rearrange("p (c i t) -> p c t i", i=4, t=PACK),
                 gated[v][:].rearrange("p t (c i) -> p c t i", i=4),
@@ -220,6 +228,10 @@ def tile_picked_twpqgatebgvar_none_po_kernel(
                 for t in range(PACK):
                     nc.scalar.activation(squares[t][:, P * side : P * (side + 1)], h_banks[side][:, t, :], ACT.Square)
 
+        kept = keep.tile([P, max(len(ON_TENSOR), 1), PACK, P], F32, name="kept", tag=f"zb{last}", align_bytes=64)
+        for at, side in enumerate(ON_TENSOR):
+            h_kept[side] = kept[:, at, :, :]
+            nc.vector.tensor_copy(h_kept[side], h_banks[side][:])
         out_rows = out_0.rearrange("(p t) j -> p t j", t=PACK)
         out_words = out_1[0].rearrange("p c r -> p (c r)").bitcast(I32)
         y_w = keep.tile([P, S], U32, name="y_w", align_bytes=64)
@@ -230,47 +242,78 @@ def tile_picked_twpqgatebgvar_none_po_kernel(
             chunks.append(slice(first, first + width))
         fetched = {}
         roots = {}
+        totals = {}
 
         def fetch(c):
             width = CHUNKS[c] * MEMBERS
             fetched[c] = keep.tile([P, PACK, width], F32, name=f"fetched{c}", tag="fetched", bufs=3)
             members = entries(n3_t, slice(chunks[c].start * MEMBERS, chunks[c].stop * MEMBERS))
             for t in range(PACK):
-                if t < (2, 2, 1, 1, 0)[c]:
+                if t < (2, 2, 2, 1, 0)[c]:
                     nc.vector.tensor_copy(fetched[c][:, t, :], squares[t][:].indirect(members))
                 else:
                     nc.scalar.activation(fetched[c][:, t, :], squares[t][:].indirect(members), ACT.Copy)
 
         def add_up(c):
             width = CHUNKS[c]
+            if c in ON_TENSOR:
+                totals[c] = psum.tile([P, PACK * P], F32, name=f"turned{c}", tag=f"bank1{ON_TENSOR.index(c) % 2}")[:]
+                for t in range(PACK):
+                    for e in range(MEMBERS):
+                        nc.tensor.matmul(
+                            totals[c][:, P * t : P * (t + 1)], fetched[c][:, t, e::MEMBERS], ident[:],
+                            start=e == 0, stop=e == MEMBERS - 1, is_transpose=True,
+                        )
+                return
             quads = fetched[c][:].rearrange("p t (j e) -> p (t j) e", e=MEMBERS)
             pairs = keep.tile([P, PACK * width, 2], F32, name=f"pairs{c}")
             nc.vector.tensor_tensor(pairs[:], quads[:, :, 0:2], quads[:, :, 2:4], ALU.add)
-            total = fetched[c][:, 0, :]
-            nc.vector.scalar_tensor_tensor(total, pairs[:, :, 0], 0.5, pairs[:, :, 1], ALU.add, ALU.add)
-            roots[c] = keep.tile([P, PACK, width], F32, name=f"root{c}")
-            nc.scalar.activation(roots[c][:].rearrange("p t j -> p (t j)"), total, ACT.Abs_reciprocal_sqrt)
+            totals[c] = fetched[c][:, 0, :]
+            nc.vector.tensor_tensor(totals[c], pairs[:, :, 0], pairs[:, :, 1], ALU.add)
+
+        def take_root(c):
+            roots[c] = keep.tile([P, PACK, CHUNKS[c]], F32, name=f"root{c}")
+            nc.scalar.activation(roots[c][:].rearrange("p t j -> p (t j)"), totals[c], ACT.Abs_reciprocal_sqrt, bias=0.5)
+
+        def turn_back(c):
+            turned = roots[c]
+            roots[c] = psum.tile([P, PACK, P], F32, name=f"back{c}", tag=f"bank1{2 + ON_TENSOR.index(c) % 2}")
+            for t in range(PACK):
+                nc.tensor.transpose(roots[c][:, t, :], turned[:, t, :], ident[:])
 
         def finish(c):
             width, cols = CHUNKS[c], chunks[c]
             side, at = divmod(cols.start, P)
             y = keep.tile([P, PACK, width], F32, name=f"y{c}")
-            nc.vector.tensor_tensor(y[:], h_banks[side][:, :, at : at + width], roots[c][:], ALU.mult)
+            if c in ON_TENSOR:
+                nc.vector.tensor_tensor(y[:], roots[c][:], h_kept[side], ALU.mult)
+            else:
+                nc.vector.tensor_tensor(y[:], h_banks[side][:, :, at : at + width], roots[c][:], ALU.mult)
             nc.sync.dma_start(out_rows[:, :, cols], y[:])
             yb = keep.tile([P, width * PACK], BF16, name=f"yb{c}", align_bytes=64)
             nc.vector.tensor_copy(
                 yb[:].rearrange("p (c i t) -> p c t i", i=4, t=PACK), y[:].rearrange("p t (c i) -> p c t i", i=4)
             )
             nc.vector.quantize_mx(out=y_w[:, cols].bitcast(FP8X4), scales=y_s[:, cols], in_=yb[:])
-            nc.sync.dma_start(out_words[:, cols], y_w[:, cols].bitcast(I32))
+            if c in (1, 4):
+                done = slice(0, 256) if c == 1 else slice(256, 512)
+                nc.sync.dma_start(out_words[:, done], y_w[:, done].bitcast(I32))
 
-        for c in range(len(CHUNKS) + 2):
-            if 1 <= c <= len(CHUNKS):
-                add_up(c - 1)
-            if c >= 2:
-                finish(c - 2)
-            if c < len(CHUNKS):
+        def due(step, near, far):
+            return [c for c in range(len(CHUNKS)) if c + (far if c in ON_TENSOR else near) == step]
+
+        for step in range(len(CHUNKS) + 4):
+            for c in due(step, 0, 0):
                 fetch(c)
+            for c in due(step, 1, 1):
+                add_up(c)
+            for c in due(step, 1, 2):
+                take_root(c)
+            for c in due(step, -9, 2):
+                turn_back(c)
+            for c in due(step, 2, 3):
+                finish(c)
+
         for q in range(4):
             queue = nc.sync if q % 2 else nc.scalar
             queue.dma_start(out_2[0, 4 * q : 4 * q + 4, :].bitcast(I32), y_s[32 * q : 32 * q + 4, :].bitcast(I32))

@@ -3,7 +3,8 @@ from contextlib import ExitStack
 import concourse.mybir as mybir
 from concourse.masks import make_identity
 
-K, T, S, N, G, H = 512, 1024, 512, 512, 2048, 512
+T, G = 1024, 2048
+S, H, N = 512, 512, 512
 FLOPS = 3 * 2 * 512 * 512 * 512
 
 F32 = mybir.dt.float32
@@ -19,13 +20,24 @@ ACT = mybir.ActivationFunctionType
 
 P = 128
 PACK = 4
-HALF = S // 2
-CHUNKS = (128, 128, 128, 64, 64,)
-PIECES = (256, 128, 128,)
-EARLY = 8
+LINE = 4
+GROUP = 16
 MEMBERS = 4
 SPARE = 16
-ON_TENSOR = (0, 1)
+
+PIECES = (256, 128, 128)
+CHUNKS = (128, 128, 128, 64, 64)
+ON_TENSOR = (0, 1, 3)
+COLUMNS_A_VECTOR_TILE = 64
+FETCH_BUFS = 3
+
+
+def spans(widths):
+    return [slice(sum(widths[:i]), sum(widths[: i + 1])) for i in range(len(widths))]
+
+
+def entries(offsets, span):
+    return offsets[:, span.start // GROUP : span.stop // GROUP]
 
 
 def tile_picked_twpqgatebgvar_none_po_kernel(
@@ -37,28 +49,15 @@ def tile_picked_twpqgatebgvar_none_po_kernel(
         psum = ctx.enter_context(tc.psum_pool(name="psum", bufs=1))
 
         def load_list(name, dram):
-            t = keep.tile(list(dram.shape), U16, name=name)
-            nc.sync.dma_start(t[:], dram)
-            return t
-
-        def zeroed_bytes(name, width, engine):
-            t = keep.tile([P, width], U8, name=name, align_bytes=64)
-            engine.memset(t[:].bitcast(I32), 0)
-            return t
-
-        def load_scale_rows(t, dram, queue):
-            for q in range(4):
-                queue.dma_start(t[32 * q : 32 * q + 4, :].bitcast(I32), dram[0, 4 * q : 4 * q + 4, :].bitcast(I32))
+            offsets = keep.tile(list(dram.shape), U16, name=name)
+            nc.sync.dma_start(offsets[:], dram)
+            return offsets
 
         def load_block_scales(name, dram, width):
-            t = keep.tile([P, width], U8, name=name)
+            table = keep.tile([P, width], U8, name=name)
             rows = dram[0].bitcast(I32).unsqueeze(1).to_broadcast([16, 8, width // 4])
-            nc.sync.dma_start(t[:].bitcast(I32), rows)
-            return t
-
-        def place_scale_rows(plane, picked):
-            for r in range(4):
-                nc.sync.dma_start(plane[r:P:32, :].bitcast(I32), picked[8 * r : P : 32, :].bitcast(I32))
+            nc.sync.dma_start(table[:].bitcast(I32), rows)
+            return table
 
         offs_t = load_list("offs_t", offs)
         x_sc = load_block_scales("x_sc", x_scales, T)
@@ -76,15 +75,18 @@ def tile_picked_twpqgatebgvar_none_po_kernel(
 
         gain = keep.tile([P, PACK], F32, name="gain")
         nc.gpsimd.dma_start(gain[:], gn.rearrange("(p t) o -> p (t o)", t=PACK))
-        w_sc = zeroed_bytes("w_sc", N, nc.gpsimd)
-        load_scale_rows(w_sc, w1_scales, nc.gpsimd)
         w_w = keep.tile([P, 2 * N], U8, name="w_w")
         nc.gpsimd.dma_start(w_w[:].bitcast(I32), w1_words[0].bitcast(I32))
-        planes = [zeroed_bytes(f"plane{u}", H + S, nc.vector) for u in range(2)]
+
+        planes = []
+        for u in range(2):
+            planes.append(keep.tile([P, H + S], U8, name=f"plane{u}", align_bytes=64))
+            nc.vector.memset(planes[u][:].bitcast(I32), 0)
 
         squares = [keep.tile([P, S + SPARE], F32, name=f"squares{t}") for t in range(PACK)]
         for t in range(PACK):
             nc.vector.memset(squares[t][:, S:], 0.0)
+
         warm = keep.tile([P, 2], F32, name="warm")
         nc.scalar.activation(warm[:, 0:1], gain[:, 0:1], ACT.Sigmoid)
 
@@ -93,8 +95,8 @@ def tile_picked_twpqgatebgvar_none_po_kernel(
         gain16 = keep.tile([P, PACK], F32, name="gain16")
         nc.scalar.activation(gain16[:], gain[:], ACT.Copy, scale=0.0625)
 
-        def coded_product(u, tokens, codes):
-            picked = keep.tile([P, H + S], U8, name=f"picked{u}", tag="picked_bytes" if u == 0 else "picked_words", align_bytes=64)
+        def gather_scales(u, tokens, codes, tag):
+            picked = keep.tile([P, H + S], U8, name=f"picked{u}", tag=tag, align_bytes=64)
             nc.vector.tensor_copy(picked[:, H:], x_sc[:].indirect(tokens[:]))
             nc.vector.tensor_copy(picked[:, :H], d_sc[:].indirect(codes[:]))
             dealt = keep.tile([P, H + S], U8, name=f"dealt{u}", tag=f"dealt{u}", align_bytes=64)
@@ -102,29 +104,23 @@ def tile_picked_twpqgatebgvar_none_po_kernel(
             nc.vector.tensor_copy(
                 dealt[:, :H].rearrange("p (t m) -> p t m", t=PACK), picked[:, :H].rearrange("p (m t) -> p t m", t=PACK)
             )
-            place_scale_rows(planes[u], dealt)
-            if u == 0:
-                xw = keep.tile([P, S], U32, name="xw0", align_bytes=64)[:]
-                dw = keep.tile([P, H], U32, name="dw0", tag="picked_words", align_bytes=64)[:]
-                nc.vector.tensor_copy(xw, x_w[:].bitcast(U32).indirect(tokens[:]))
-                nc.vector.tensor_copy(dw, d_w[:].bitcast(U32).indirect(codes[:]))
-            else:
-                both = keep.tile([P, H + S], U32, name="both", tag="picked_words", align_bytes=64)
-                dw, xw = both[:, :H], both[:, H:]
-                nc.vector.tensor_copy(dw, d_w[:].bitcast(U32).indirect(codes[:]))
-                nc.vector.tensor_copy(xw, x_w[:].bitcast(U32).indirect(tokens[:]))
-            dwd = keep.tile([P, H], U32, name=f"dwd{u}", align_bytes=64)
+            for r in range(4):
+                nc.sync.dma_start(planes[u][r:P:32, :].bitcast(I32), dealt[8 * r : P : 32, :].bitcast(I32))
+
+        def multiply(u, code_words, token_words):
+            dealt_words = keep.tile([P, H], U32, name=f"dealt_words{u}", align_bytes=64)
             nc.vector.tensor_copy(
-                dwd[:].rearrange("p (t c i) -> p c t i", t=PACK, i=4), dw.rearrange("p (c i t) -> p c t i", t=PACK, i=4)
+                dealt_words[:].rearrange("p (t c i) -> p c t i", t=PACK, i=LINE),
+                code_words.rearrange("p (c i t) -> p c t i", t=PACK, i=LINE),
             )
             banks = []
             for t in range(PACK):
                 bank = psum.tile([P, S], F32, name=f"bank{u}{t}", tag=f"bank{u}{t}")
                 nc.tensor.matmul_mx(
                     out=bank[:],
-                    lhsT=dwd[:, P * t : P * (t + 1)].bitcast(FP8X4),
+                    lhsT=dealt_words[:, P * t : P * (t + 1)].bitcast(FP8X4),
                     lhsT_scale=planes[u][:, P * t : P * (t + 1)],
-                    rhs=xw.bitcast(FP8X4),
+                    rhs=token_words.bitcast(FP8X4),
                     rhs_scale=planes[u][:, H:],
                     start=True,
                     stop=True,
@@ -132,188 +128,191 @@ def tile_picked_twpqgatebgvar_none_po_kernel(
                 banks.append(bank)
             return banks
 
-        a_banks = coded_product(0, offs_t, k1_t)
+        gather_scales(0, offs_t, k1_t, "picked_a")
+        a_tokens = keep.tile([P, S], U32, name="a_tokens", align_bytes=64)
+        a_codes = keep.tile([P, H], U32, name="a_codes", tag="picked", align_bytes=64)
+        nc.vector.tensor_copy(a_tokens[:], x_w[:].bitcast(U32).indirect(offs_t[:]))
+        nc.vector.tensor_copy(a_codes[:], d_w[:].bitcast(U32).indirect(k1_t[:]))
+        a_banks = multiply(0, a_codes[:], a_tokens[:])
         ga = [keep.tile([P, S], F32, name=f"ga{t}") for t in range(PACK)]
         for t in range(PACK):
             nc.scalar.activation(ga[t][:], a_banks[t][:], ACT.Copy, scale=gain16[:, t : t + 1])
 
-        b_banks = coded_product(1, two_t, k2_t)
+        w_sc = keep.tile([P, N], U8, name="w_sc", tag="picked_a", align_bytes=64)
+        nc.gpsimd.memset(w_sc[:].bitcast(I32), 0)
+        for q in range(4):
+            nc.sync.dma_start(w_sc[32 * q : 32 * q + 4, :].bitcast(I32), w1_scales[0, 4 * q : 4 * q + 4, :].bitcast(I32))
 
-        w_sd = keep.tile([P, N], U8, name="w_sd", tag="dealt1", align_bytes=64)
+        gather_scales(1, two_t, k2_t, "picked")
+        b_words = keep.tile([P, H + S], U32, name="b_words", tag="picked", align_bytes=64)
+        nc.vector.tensor_copy(b_words[:, :H], d_w[:].bitcast(U32).indirect(k2_t[:]))
+        nc.vector.tensor_copy(b_words[:, H:], x_w[:].bitcast(U32).indirect(two_t[:]))
+        b_banks = multiply(1, b_words[:, :H], b_words[:, H:])
+
+        w_plane = keep.tile([P, N], U8, name="w_plane", tag="dealt1", align_bytes=64)
         nc.vector.tensor_copy(
-            w_sd[:].rearrange("p (t m) -> p t m", t=PACK), w_sc[:].rearrange("p (m t) -> p t m", t=PACK)
+            w_plane[:].rearrange("p (t m) -> p t m", t=PACK), w_sc[:].rearrange("p (m t) -> p t m", t=PACK)
         )
 
-        pieces = []
-        for width in PIECES:
-            first = sum(PIECES[: len(pieces)])
-            pieces.append(slice(first, first + width))
+        pieces = spans(PIECES)
         last = len(PIECES) - 1
         half_ga = [
-            keep.tile([P, PACK, w], F32, name=f"half_ga{v}", tag="x_w" if v == last else f"half_ga{v}")
-            for v, w in enumerate(PIECES)
+            keep.tile([P, PACK, width], F32, name=f"half_ga{v}", tag="x_w" if v == last else f"half_ga{v}")
+            for v, width in enumerate(PIECES)
         ]
-        gated = {}
-        fetched_gate = {}
         gate = [keep.tile([P, S], F32, name=f"gate{t}") for t in range(PACK)]
-
-        def entries(lst, cols):
-            return lst[:, cols.start // 16 : cols.stop // 16]
-
-        jobs = [(v, t) for v in range(len(PIECES)) for t in range(PACK)]
-
-        def fetch_half_ga(some):
-            for v, t in some:
-                looked_up = ga[t][:].indirect(entries(n1_t, pieces[v]))
-                if v == last and t < 4:
-                    nc.vector.tensor_scalar(half_ga[v][:, t, :], looked_up, 0.5, 0.0, ALU.mult, ALU.add)
-                else:
-                    nc.scalar.activation(half_ga[v][:, t, :], looked_up, ACT.Copy, scale=0.5)
-
-        fetch_half_ga(jobs[:EARLY])
+        for v in range(last):
+            for t in range(PACK):
+                nc.scalar.activation(half_ga[v][:, t, :], ga[t][:].indirect(entries(n1_t, pieces[v])), ACT.Copy, scale=0.5)
         for t in range(PACK):
             nc.scalar.activation(gate[t][:], b_banks[t][:], ACT.Sigmoid, scale=0.0625)
-        fetch_half_ga(jobs[EARLY:])
+        for t in range(PACK):
+            nc.vector.tensor_scalar(
+                half_ga[last][:, t, :], ga[t][:].indirect(entries(n1_t, pieces[last])), 0.5, 0.0, ALU.mult, ALU.add
+            )
 
-        w_wd = keep.tile([P, 2 * N], U8, name="w_wd", align_bytes=64)
-        h_banks = {}
-        h_kept = {}
-        def mix(v, t):
-            if t == 0:
-                gated[v] = keep.tile([P, PACK, PIECES[v]], F32, name=f"gated{v}", tag="gated", bufs=2)
-            looked_up = gate[t][:].indirect(entries(n2_t, pieces[v]))
-            if v >= 1:
-                if v == 1:
-                    rest = slice(PIECES[0], S)
-                    fetched_gate[t] = keep.tile([P, S - PIECES[0]], F32, name=f"fetched_gate{t}")
-                    nc.scalar.activation(fetched_gate[t][:], gate[t][:].indirect(entries(n2_t, rest)), ACT.Copy)
-                looked_up = fetched_gate[t][:, pieces[v].start - PIECES[0] : pieces[v].stop - PIECES[0]]
-            nc.vector.tensor_tensor(gated[v][:, t, :], looked_up, ga[t][:, pieces[v]], ALU.mult)
-            return looked_up
-
+        w_dealt = keep.tile([P, 2 * N], U8, name="w_dealt", align_bytes=64)
         nc.scalar.copy(
-            w_wd[:].bitcast(U16).rearrange("p (t m) -> p t m", t=PACK),
+            w_dealt[:].bitcast(U16).rearrange("p (t m) -> p t m", t=PACK),
             w_w[:].bitcast(U16).rearrange("p (m t) -> p t m", t=PACK),
         )
 
+        later = slice(PIECES[0], S)
+        later_gates = []
+        h_banks = []
         for v, cols in enumerate(pieces):
             width = PIECES[v]
+            gated = keep.tile([P, PACK, width], F32, name=f"gated{v}", tag="gated", bufs=2)
             for t in range(PACK):
-                newest = mix(v, t)
+                if v == 0:
+                    gates = gate[t][:].indirect(entries(n2_t, cols))
+                else:
+                    if cols.start == later.start:
+                        later_gates.append(keep.tile([P, S - later.start], F32, name=f"later_gates{t}"))
+                        nc.scalar.activation(later_gates[t][:], gate[t][:].indirect(entries(n2_t, later)), ACT.Copy)
+                    gates = later_gates[t][:, cols.start - later.start : cols.stop - later.start]
+                nc.vector.tensor_tensor(gated[:, t, :], gates, ga[t][:, cols], ALU.mult)
             if v == last:
-                nc.scalar.activation(warm[:, 1:2], newest[:, 0:1], ACT.Abs_reciprocal_sqrt, bias=0.5)
-            zb = keep.tile([P, width * PACK], BF16, name=f"zb{v}", tag=f"zb{v}", align_bytes=64)
+                nc.scalar.activation(warm[:, 1:2], gates[:, 0:1], ACT.Abs_reciprocal_sqrt, bias=0.5)
+            z_rounded = keep.tile([P, width * PACK], BF16, name=f"z_rounded{v}", tag=f"z_rounded{v}", align_bytes=64)
             nc.vector.tensor_tensor(
-                zb[:].rearrange("p (c i t) -> p c t i", i=4, t=PACK),
-                gated[v][:].rearrange("p t (c i) -> p c t i", i=4),
-                half_ga[v][:].rearrange("p t (c i) -> p c t i", i=4),
+                z_rounded[:].rearrange("p (c i t) -> p c t i", i=LINE, t=PACK),
+                gated[:].rearrange("p t (c i) -> p c t i", i=LINE),
+                half_ga[v][:].rearrange("p t (c i) -> p c t i", i=LINE),
                 ALU.subtract,
             )
-            zw = keep.tile([P, width], U32, name=f"zw{v}", align_bytes=64)
-            zs = keep.tile([P, width], U8, name=f"zs{v}", align_bytes=64)
-            nc.vector.quantize_mx(out=zw[:].bitcast(FP8X4), scales=zs[:], in_=zb[:])
+            z_words = keep.tile([P, width], U32, name=f"z_words{v}", align_bytes=64)
+            z_plane = keep.tile([P, width], U8, name=f"z_plane{v}", align_bytes=64)
+            nc.vector.quantize_mx(out=z_words[:].bitcast(FP8X4), scales=z_plane[:], in_=z_rounded[:])
             for at in range(0, width, P):
-                side = (cols.start + at) // P
-                h_banks[side] = psum.tile([P, PACK, P], F32, name=f"h{side}", tag=f"bank0{side}")
+                s = (cols.start + at) // P
+                h_banks.append(psum.tile([P, PACK, P], F32, name=f"h{s}", tag=f"bank0{s}"))
                 for t in range(PACK):
                     nc.tensor.matmul_mx(
-                        out=h_banks[side][:, t, :],
-                        lhsT=w_wd[:, 2 * P * t : 2 * P * (t + 1)].bitcast(FP4X4),
-                        lhsT_scale=w_sd[:, P * t : P * (t + 1)],
-                        rhs=zw[:, at : at + P].bitcast(FP8X4),
-                        rhs_scale=zs[:, at : at + P],
+                        out=h_banks[s][:, t, :],
+                        lhsT=w_dealt[:, 2 * P * t : 2 * P * (t + 1)].bitcast(FP4X4),
+                        lhsT_scale=w_plane[:, P * t : P * (t + 1)],
+                        rhs=z_words[:, at : at + P].bitcast(FP8X4),
+                        rhs_scale=z_plane[:, at : at + P],
                         start=True,
                         stop=True,
                     )
                 for t in range(PACK):
-                    nc.scalar.activation(squares[t][:, P * side : P * (side + 1)], h_banks[side][:, t, :], ACT.Square)
+                    nc.scalar.activation(squares[t][:, P * s : P * (s + 1)], h_banks[s][:, t, :], ACT.Square)
 
-        kept = keep.tile([P, max(len(ON_TENSOR), 1), PACK, P], F32, name="kept", tag=f"zb{last}", align_bytes=64)
-        for at, side in enumerate(ON_TENSOR):
-            h_kept[side] = kept[:, at, :, :]
-            nc.vector.tensor_copy(h_kept[side], h_banks[side][:])
+        chunks = spans(CHUNKS)
+
+        def h_in_psum(c):
+            s, at = divmod(chunks[c].start, P)
+            return h_banks[s][:, :, at : at + CHUNKS[c]]
+
+        kept = keep.tile([P, len(ON_TENSOR), PACK, P], F32, name="kept", tag=f"z_rounded{last}", align_bytes=64)
+        h_kept = {}
+        for i, c in enumerate(ON_TENSOR):
+            h_kept[c] = kept[:, i, :, : CHUNKS[c]]
+            nc.vector.tensor_copy(h_kept[c], h_in_psum(c))
+
         out_rows = out_0.rearrange("(p t) j -> p t j", t=PACK)
         out_words = out_1[0].rearrange("p c r -> p (c r)").bitcast(I32)
-        y_w = keep.tile([P, S], U32, name="y_w", align_bytes=64)
-        y_s = keep.tile([P, S], U8, name="y_s", align_bytes=64)
-        chunks = []
-        for width in CHUNKS:
-            first = sum(CHUNKS[: len(chunks)])
-            chunks.append(slice(first, first + width))
-        fetched = {}
-        roots = {}
-        totals = {}
+        y_words = keep.tile([P, S], U32, name="y_words", align_bytes=64)
+        y_plane = keep.tile([P, S], U8, name="y_plane", align_bytes=64)
+        fetched, totals, roots = {}, {}, {}
 
         def fetch(c):
-            width = CHUNKS[c] * MEMBERS
-            fetched[c] = keep.tile([P, PACK, width], F32, name=f"fetched{c}", tag="fetched", bufs=3)
+            fetched[c] = keep.tile([P, PACK, CHUNKS[c] * MEMBERS], F32, name=f"fetched{c}", tag="fetched", bufs=FETCH_BUFS)
             members = entries(n3_t, slice(chunks[c].start * MEMBERS, chunks[c].stop * MEMBERS))
             for t in range(PACK):
-                if t < (2, 2, 2, 1, 0)[c]:
+                if t < CHUNKS[c] // COLUMNS_A_VECTOR_TILE:
                     nc.vector.tensor_copy(fetched[c][:, t, :], squares[t][:].indirect(members))
                 else:
                     nc.scalar.activation(fetched[c][:, t, :], squares[t][:].indirect(members), ACT.Copy)
 
         def add_up(c):
-            width = CHUNKS[c]
+            count = PACK * CHUNKS[c]
+            quads = fetched[c][:].rearrange("p t (j e) -> p (t j) e", e=MEMBERS)
             if c in ON_TENSOR:
-                totals[c] = psum.tile([P, PACK * P], F32, name=f"turned{c}", tag=f"bank1{ON_TENSOR.index(c) % 2}")[:]
-                for t in range(PACK):
+                totals[c] = psum.tile([P, count], F32, name=f"turned{c}", tag=f"bank1{ON_TENSOR.index(c) % 2}")[:]
+                for at in range(0, count, P):
                     for e in range(MEMBERS):
                         nc.tensor.matmul(
-                            totals[c][:, P * t : P * (t + 1)], fetched[c][:, t, e::MEMBERS], ident[:],
-                            start=e == 0, stop=e == MEMBERS - 1, is_transpose=True,
+                            totals[c][:, at : at + P],
+                            quads[:, at : at + P, e],
+                            ident[:],
+                            start=e == 0,
+                            stop=e == MEMBERS - 1,
+                            is_transpose=True,
                         )
-                return
-            quads = fetched[c][:].rearrange("p t (j e) -> p (t j) e", e=MEMBERS)
-            pairs = keep.tile([P, PACK * width, 2], F32, name=f"pairs{c}")
-            nc.vector.tensor_tensor(pairs[:], quads[:, :, 0:2], quads[:, :, 2:4], ALU.add)
-            totals[c] = fetched[c][:, 0, :]
-            nc.vector.tensor_tensor(totals[c], pairs[:, :, 0], pairs[:, :, 1], ALU.add)
+            else:
+                pairs = keep.tile([P, count, 2], F32, name=f"pairs{c}")
+                nc.vector.tensor_tensor(pairs[:], quads[:, :, 0:2], quads[:, :, 2:4], ALU.add)
+                totals[c] = fetched[c][:, 0, :]
+                nc.vector.tensor_tensor(totals[c], pairs[:, :, 0], pairs[:, :, 1], ALU.add)
 
         def take_root(c):
             roots[c] = keep.tile([P, PACK, CHUNKS[c]], F32, name=f"root{c}")
             nc.scalar.activation(roots[c][:].rearrange("p t j -> p (t j)"), totals[c], ACT.Abs_reciprocal_sqrt, bias=0.5)
 
         def turn_back(c):
-            turned = roots[c]
-            roots[c] = psum.tile([P, PACK, P], F32, name=f"back{c}", tag=f"bank1{2 + ON_TENSOR.index(c) % 2}")
-            for t in range(PACK):
-                nc.tensor.transpose(roots[c][:, t, :], turned[:, t, :], ident[:])
+            turned = roots[c][:].rearrange("p t j -> p (t j)")
+            roots[c] = psum.tile([P, PACK, CHUNKS[c]], F32, name=f"back{c}", tag=f"bank1{2 + ON_TENSOR.index(c) % 2}")
+            back = roots[c][:].rearrange("p t j -> p (t j)")
+            for at in range(0, PACK * CHUNKS[c], P):
+                nc.tensor.transpose(back[:, at : at + P], turned[:, at : at + P], ident[:])
 
         def finish(c):
             width, cols = CHUNKS[c], chunks[c]
-            side, at = divmod(cols.start, P)
             y = keep.tile([P, PACK, width], F32, name=f"y{c}")
             if c in ON_TENSOR:
-                nc.vector.tensor_tensor(y[:], roots[c][:], h_kept[side], ALU.mult)
+                nc.vector.tensor_tensor(y[:], roots[c][:], h_kept[c], ALU.mult)
             else:
-                nc.vector.tensor_tensor(y[:], h_banks[side][:, :, at : at + width], roots[c][:], ALU.mult)
+                nc.vector.tensor_tensor(y[:], h_in_psum(c), roots[c][:], ALU.mult)
             nc.sync.dma_start(out_rows[:, :, cols], y[:])
-            yb = keep.tile([P, width * PACK], BF16, name=f"yb{c}", align_bytes=64)
+            y_rounded = keep.tile([P, width * PACK], BF16, name=f"y_rounded{c}", align_bytes=64)
             nc.vector.tensor_copy(
-                yb[:].rearrange("p (c i t) -> p c t i", i=4, t=PACK), y[:].rearrange("p t (c i) -> p c t i", i=4)
+                y_rounded[:].rearrange("p (c i t) -> p c t i", i=LINE, t=PACK),
+                y[:].rearrange("p t (c i) -> p c t i", i=LINE),
             )
-            nc.vector.quantize_mx(out=y_w[:, cols].bitcast(FP8X4), scales=y_s[:, cols], in_=yb[:])
-            if c in (1, 4):
-                done = slice(0, 256) if c == 1 else slice(256, 512)
-                nc.sync.dma_start(out_words[:, done], y_w[:, done].bitcast(I32))
+            nc.vector.quantize_mx(out=y_words[:, cols].bitcast(FP8X4), scales=y_plane[:, cols], in_=y_rounded[:])
+            if cols.stop % (S // 2) == 0:
+                half = slice(cols.stop - S // 2, cols.stop)
+                nc.sync.dma_start(out_words[:, half], y_words[:, half].bitcast(I32))
 
-        def due(step, near, far):
-            return [c for c in range(len(CHUNKS)) if c + (far if c in ON_TENSOR else near) == step]
-
-        for step in range(len(CHUNKS) + 4):
-            for c in due(step, 0, 0):
-                fetch(c)
-            for c in due(step, 1, 1):
-                add_up(c)
-            for c in due(step, 1, 2):
+        root_step = [c + 1 + (c in ON_TENSOR) for c in range(len(CHUNKS))]
+        for step in range(max(root_step) + 2):
+            if step < len(CHUNKS):
+                fetch(step)
+            if 1 <= step <= len(CHUNKS):
+                add_up(step - 1)
+            rooted = [c for c in range(len(CHUNKS)) if root_step[c] == step]
+            for c in rooted:
                 take_root(c)
-            for c in due(step, -9, 2):
-                turn_back(c)
-            for c in due(step, 2, 3):
-                finish(c)
+            for c in rooted:
+                if c in ON_TENSOR:
+                    turn_back(c)
+            for c in range(len(CHUNKS)):
+                if root_step[c] + 1 == step:
+                    finish(c)
 
         for q in range(4):
             queue = nc.sync if q % 2 else nc.scalar
-            queue.dma_start(out_2[0, 4 * q : 4 * q + 4, :].bitcast(I32), y_s[32 * q : 32 * q + 4, :].bitcast(I32))
+            queue.dma_start(out_2[0, 4 * q : 4 * q + 4, :].bitcast(I32), y_plane[32 * q : 32 * q + 4, :].bitcast(I32))

from contextlib import ExitStack

import concourse.mybir as mybir
from concourse.masks import make_identity

T, G = 1024, 2048
S, H, N = 512, 512, 512
FLOPS = 3 * 2 * 512 * 512 * 512

F32 = mybir.dt.float32
BF16 = mybir.dt.bfloat16
I32 = mybir.dt.int32
U32 = mybir.dt.uint32
U16 = mybir.dt.uint16
U8 = mybir.dt.uint8
FP8X4 = mybir.dt.float8_e4m3fn_x4
FP4X4 = mybir.dt.float4_e2m1fn_x4
ALU = mybir.AluOpType
ACT = mybir.ActivationFunctionType

P = 128
PACK = 4
LINE = 4
GROUP = 16
MEMBERS = 4
SPARE = 16

PIECES = (256, 128, 128)
CHUNKS = (128, 128, 128, 64, 64)
ON_TENSOR = (0, 1, 3)
COLUMNS_A_VECTOR_TILE = 64
FETCH_BUFS = 3


def spans(widths):
    return [slice(sum(widths[:i]), sum(widths[: i + 1])) for i in range(len(widths))]


def entries(offsets, span):
    return offsets[:, span.start // GROUP : span.stop // GROUP]


def tile_picked_twpqgatebgvar_none_po_kernel(
    tc, x_words, x_scales, d_words, d_scales, gn, w1_words, w1_scales, offs, k1, two, k2, n1, n2, n3, out_0, out_1, out_2
):
    nc = tc.nc
    with ExitStack() as ctx:
        keep = ctx.enter_context(tc.tile_pool(name="keep", bufs=1))
        psum = ctx.enter_context(tc.psum_pool(name="psum", bufs=1))

        def load_list(name, dram):
            offsets = keep.tile(list(dram.shape), U16, name=name)
            nc.sync.dma_start(offsets[:], dram)
            return offsets

        def load_block_scales(name, dram, width):
            table = keep.tile([P, width], U8, name=name)
            rows = dram[0].bitcast(I32).unsqueeze(1).to_broadcast([16, 8, width // 4])
            nc.sync.dma_start(table[:].bitcast(I32), rows)
            return table

        offs_t = load_list("offs_t", offs)
        x_sc = load_block_scales("x_sc", x_scales, T)
        k1_t = load_list("k1_t", k1)
        d_sc = load_block_scales("d_sc", d_scales, G)
        x_w = keep.tile([P, T], I32, name="x_w", tag="x_w")
        nc.sync.dma_start(x_w[:], x_words[0].rearrange("p c r -> p (c r)").bitcast(I32))
        k2_t = load_list("k2_t", k2)
        two_t = load_list("two_t", two)
        d_w = keep.tile([P, G], I32, name="d_w")
        nc.sync.dma_start(d_w[:], d_words[0].rearrange("p c r -> p (c r)").bitcast(I32))
        n1_t = load_list("n1_t", n1)
        n2_t = load_list("n2_t", n2)
        n3_t = load_list("n3_t", n3)

        gain = keep.tile([P, PACK], F32, name="gain")
        nc.gpsimd.dma_start(gain[:], gn.rearrange("(p t) o -> p (t o)", t=PACK))
        w_w = keep.tile([P, 2 * N], U8, name="w_w")
        nc.gpsimd.dma_start(w_w[:].bitcast(I32), w1_words[0].bitcast(I32))

        planes = []
        for u in range(2):
            planes.append(keep.tile([P, H + S], U8, name=f"plane{u}", align_bytes=64))
            nc.vector.memset(planes[u][:].bitcast(I32), 0)

        squares = [keep.tile([P, S + SPARE], F32, name=f"squares{t}") for t in range(PACK)]
        for t in range(PACK):
            nc.vector.memset(squares[t][:, S:], 0.0)

        warm = keep.tile([P, 2], F32, name="warm")
        nc.scalar.activation(warm[:, 0:1], gain[:, 0:1], ACT.Sigmoid)

        ident = keep.tile([P, P], F32, name="ident")
        make_identity(nc, ident[:])
        gain16 = keep.tile([P, PACK], F32, name="gain16")
        nc.scalar.activation(gain16[:], gain[:], ACT.Copy, scale=0.0625)

        def gather_scales(u, tokens, codes, tag):
            picked = keep.tile([P, H + S], U8, name=f"picked{u}", tag=tag, align_bytes=64)
            nc.vector.tensor_copy(picked[:, H:], x_sc[:].indirect(tokens[:]))
            nc.vector.tensor_copy(picked[:, :H], d_sc[:].indirect(codes[:]))
            dealt = keep.tile([P, H + S], U8, name=f"dealt{u}", tag=f"dealt{u}", align_bytes=64)
            nc.vector.tensor_copy(dealt[:, H:].bitcast(I32), picked[:, H:].bitcast(I32))
            nc.vector.tensor_copy(
                dealt[:, :H].rearrange("p (t m) -> p t m", t=PACK), picked[:, :H].rearrange("p (m t) -> p t m", t=PACK)
            )
            for r in range(4):
                nc.sync.dma_start(planes[u][r:P:32, :].bitcast(I32), dealt[8 * r : P : 32, :].bitcast(I32))

        def multiply(u, code_words, token_words):
            dealt_words = keep.tile([P, H], U32, name=f"dealt_words{u}", align_bytes=64)
            nc.vector.tensor_copy(
                dealt_words[:].rearrange("p (t c i) -> p c t i", t=PACK, i=LINE),
                code_words.rearrange("p (c i t) -> p c t i", t=PACK, i=LINE),
            )
            banks = []
            for t in range(PACK):
                bank = psum.tile([P, S], F32, name=f"bank{u}{t}", tag=f"bank{u}{t}")
                nc.tensor.matmul_mx(
                    out=bank[:],
                    lhsT=dealt_words[:, P * t : P * (t + 1)].bitcast(FP8X4),
                    lhsT_scale=planes[u][:, P * t : P * (t + 1)],
                    rhs=token_words.bitcast(FP8X4),
                    rhs_scale=planes[u][:, H:],
                    start=True,
                    stop=True,
                )
                banks.append(bank)
            return banks

        gather_scales(0, offs_t, k1_t, "picked_a")
        a_tokens = keep.tile([P, S], U32, name="a_tokens", align_bytes=64)
        a_codes = keep.tile([P, H], U32, name="a_codes", tag="picked", align_bytes=64)
        nc.vector.tensor_copy(a_tokens[:], x_w[:].bitcast(U32).indirect(offs_t[:]))
        nc.vector.tensor_copy(a_codes[:], d_w[:].bitcast(U32).indirect(k1_t[:]))
        a_banks = multiply(0, a_codes[:], a_tokens[:])
        ga = [keep.tile([P, S], F32, name=f"ga{t}") for t in range(PACK)]
        for t in range(PACK):
            nc.scalar.activation(ga[t][:], a_banks[t][:], ACT.Copy, scale=gain16[:, t : t + 1])

        w_sc = keep.tile([P, N], U8, name="w_sc", tag="picked_a", align_bytes=64)
        nc.gpsimd.memset(w_sc[:].bitcast(I32), 0)
        for q in range(4):
            nc.sync.dma_start(w_sc[32 * q : 32 * q + 4, :].bitcast(I32), w1_scales[0, 4 * q : 4 * q + 4, :].bitcast(I32))

        gather_scales(1, two_t, k2_t, "picked")
        b_words = keep.tile([P, H + S], U32, name="b_words", tag="picked", align_bytes=64)
        nc.vector.tensor_copy(b_words[:, :H], d_w[:].bitcast(U32).indirect(k2_t[:]))
        nc.vector.tensor_copy(b_words[:, H:], x_w[:].bitcast(U32).indirect(two_t[:]))
        b_banks = multiply(1, b_words[:, :H], b_words[:, H:])

        w_plane = keep.tile([P, N], U8, name="w_plane", tag="dealt1", align_bytes=64)
        nc.vector.tensor_copy(
            w_plane[:].rearrange("p (t m) -> p t m", t=PACK), w_sc[:].rearrange("p (m t) -> p t m", t=PACK)
        )

        pieces = spans(PIECES)
        last = len(PIECES) - 1
        half_ga = [
            keep.tile([P, PACK, width], F32, name=f"half_ga{v}", tag="x_w" if v == last else f"half_ga{v}")
            for v, width in enumerate(PIECES)
        ]
        gate = [keep.tile([P, S], F32, name=f"gate{t}") for t in range(PACK)]
        for v in range(last):
            for t in range(PACK):
                nc.scalar.activation(half_ga[v][:, t, :], ga[t][:].indirect(entries(n1_t, pieces[v])), ACT.Copy, scale=0.5)
        for t in range(PACK):
            nc.scalar.activation(gate[t][:], b_banks[t][:], ACT.Sigmoid, scale=0.0625)
        for t in range(PACK):
            nc.vector.tensor_scalar(
                half_ga[last][:, t, :], ga[t][:].indirect(entries(n1_t, pieces[last])), 0.5, 0.0, ALU.mult, ALU.add
            )

        w_dealt = keep.tile([P, 2 * N], U8, name="w_dealt", align_bytes=64)
        nc.scalar.copy(
            w_dealt[:].bitcast(U16).rearrange("p (t m) -> p t m", t=PACK),
            w_w[:].bitcast(U16).rearrange("p (m t) -> p t m", t=PACK),
        )

        later = slice(PIECES[0], S)
        later_gates = []
        h_banks = []
        for v, cols in enumerate(pieces):
            width = PIECES[v]
            gated = keep.tile([P, PACK, width], F32, name=f"gated{v}", tag="gated", bufs=2)
            for t in range(PACK):
                if v == 0:
                    gates = gate[t][:].indirect(entries(n2_t, cols))
                else:
                    if cols.start == later.start:
                        later_gates.append(keep.tile([P, S - later.start], F32, name=f"later_gates{t}"))
                        nc.scalar.activation(later_gates[t][:], gate[t][:].indirect(entries(n2_t, later)), ACT.Copy)
                    gates = later_gates[t][:, cols.start - later.start : cols.stop - later.start]
                nc.vector.tensor_tensor(gated[:, t, :], gates, ga[t][:, cols], ALU.mult)
            if v == last:
                nc.scalar.activation(warm[:, 1:2], gates[:, 0:1], ACT.Abs_reciprocal_sqrt, bias=0.5)
            z_rounded = keep.tile([P, width * PACK], BF16, name=f"z_rounded{v}", tag=f"z_rounded{v}", align_bytes=64)
            nc.vector.tensor_tensor(
                z_rounded[:].rearrange("p (c i t) -> p c t i", i=LINE, t=PACK),
                gated[:].rearrange("p t (c i) -> p c t i", i=LINE),
                half_ga[v][:].rearrange("p t (c i) -> p c t i", i=LINE),
                ALU.subtract,
            )
            z_words = keep.tile([P, width], U32, name=f"z_words{v}", align_bytes=64)
            z_plane = keep.tile([P, width], U8, name=f"z_plane{v}", align_bytes=64)
            nc.vector.quantize_mx(out=z_words[:].bitcast(FP8X4), scales=z_plane[:], in_=z_rounded[:])
            for at in range(0, width, P):
                s = (cols.start + at) // P
                h_banks.append(psum.tile([P, PACK, P], F32, name=f"h{s}", tag=f"bank0{s}"))
                for t in range(PACK):
                    nc.tensor.matmul_mx(
                        out=h_banks[s][:, t, :],
                        lhsT=w_dealt[:, 2 * P * t : 2 * P * (t + 1)].bitcast(FP4X4),
                        lhsT_scale=w_plane[:, P * t : P * (t + 1)],
                        rhs=z_words[:, at : at + P].bitcast(FP8X4),
                        rhs_scale=z_plane[:, at : at + P],
                        start=True,
                        stop=True,
                    )
                for t in range(PACK):
                    nc.scalar.activation(squares[t][:, P * s : P * (s + 1)], h_banks[s][:, t, :], ACT.Square)

        chunks = spans(CHUNKS)

        def h_in_psum(c):
            s, at = divmod(chunks[c].start, P)
            return h_banks[s][:, :, at : at + CHUNKS[c]]

        kept = keep.tile([P, len(ON_TENSOR), PACK, P], F32, name="kept", tag=f"z_rounded{last}", align_bytes=64)
        h_kept = {}
        for i, c in enumerate(ON_TENSOR):
            h_kept[c] = kept[:, i, :, : CHUNKS[c]]
            nc.vector.tensor_copy(h_kept[c], h_in_psum(c))

        out_rows = out_0.rearrange("(p t) j -> p t j", t=PACK)
        out_words = out_1[0].rearrange("p c r -> p (c r)").bitcast(I32)
        y_words = keep.tile([P, S], U32, name="y_words", align_bytes=64)
        y_plane = keep.tile([P, S], U8, name="y_plane", align_bytes=64)
        fetched, totals, roots = {}, {}, {}

        def fetch(c):
            fetched[c] = keep.tile([P, PACK, CHUNKS[c] * MEMBERS], F32, name=f"fetched{c}", tag="fetched", bufs=FETCH_BUFS)
            members = entries(n3_t, slice(chunks[c].start * MEMBERS, chunks[c].stop * MEMBERS))
            for t in range(PACK):
                if t < CHUNKS[c] // COLUMNS_A_VECTOR_TILE:
                    nc.vector.tensor_copy(fetched[c][:, t, :], squares[t][:].indirect(members))
                else:
                    nc.scalar.activation(fetched[c][:, t, :], squares[t][:].indirect(members), ACT.Copy)

        def add_up(c):
            count = PACK * CHUNKS[c]
            quads = fetched[c][:].rearrange("p t (j e) -> p (t j) e", e=MEMBERS)
            if c in ON_TENSOR:
                totals[c] = psum.tile([P, count], F32, name=f"turned{c}", tag=f"bank1{ON_TENSOR.index(c) % 2}")[:]
                for at in range(0, count, P):
                    for e in range(MEMBERS):
                        nc.tensor.matmul(
                            totals[c][:, at : at + P],
                            quads[:, at : at + P, e],
                            ident[:],
                            start=e == 0,
                            stop=e == MEMBERS - 1,
                            is_transpose=True,
                        )
            else:
                pairs = keep.tile([P, count, 2], F32, name=f"pairs{c}")
                nc.vector.tensor_tensor(pairs[:], quads[:, :, 0:2], quads[:, :, 2:4], ALU.add)
                totals[c] = fetched[c][:, 0, :]
                nc.vector.tensor_tensor(totals[c], pairs[:, :, 0], pairs[:, :, 1], ALU.add)

        def take_root(c):
            roots[c] = keep.tile([P, PACK, CHUNKS[c]], F32, name=f"root{c}")
            nc.scalar.activation(roots[c][:].rearrange("p t j -> p (t j)"), totals[c], ACT.Abs_reciprocal_sqrt, bias=0.5)

        def turn_back(c):
            turned = roots[c][:].rearrange("p t j -> p (t j)")
            roots[c] = psum.tile([P, PACK, CHUNKS[c]], F32, name=f"back{c}", tag=f"bank1{2 + ON_TENSOR.index(c) % 2}")
            back = roots[c][:].rearrange("p t j -> p (t j)")
            for at in range(0, PACK * CHUNKS[c], P):
                nc.tensor.transpose(back[:, at : at + P], turned[:, at : at + P], ident[:])

        def finish(c):
            width, cols = CHUNKS[c], chunks[c]
            y = keep.tile([P, PACK, width], F32, name=f"y{c}")
            if c in ON_TENSOR:
                nc.vector.tensor_tensor(y[:], roots[c][:], h_kept[c], ALU.mult)
            else:
                nc.vector.tensor_tensor(y[:], h_in_psum(c), roots[c][:], ALU.mult)
            nc.sync.dma_start(out_rows[:, :, cols], y[:])
            y_rounded = keep.tile([P, width * PACK], BF16, name=f"y_rounded{c}", align_bytes=64)
            nc.vector.tensor_copy(
                y_rounded[:].rearrange("p (c i t) -> p c t i", i=LINE, t=PACK),
                y[:].rearrange("p t (c i) -> p c t i", i=LINE),
            )
            nc.vector.quantize_mx(out=y_words[:, cols].bitcast(FP8X4), scales=y_plane[:, cols], in_=y_rounded[:])
            if cols.stop % (S // 2) == 0:
                half = slice(cols.stop - S // 2, cols.stop)
                nc.sync.dma_start(out_words[:, half], y_words[:, half].bitcast(I32))

        root_step = [c + 1 + (c in ON_TENSOR) for c in range(len(CHUNKS))]
        for step in range(max(root_step) + 2):
            if step < len(CHUNKS):
                fetch(step)
            if 1 <= step <= len(CHUNKS):
                add_up(step - 1)
            rooted = [c for c in range(len(CHUNKS)) if root_step[c] == step]
            for c in rooted:
                take_root(c)
            for c in rooted:
                if c in ON_TENSOR:
                    turn_back(c)
            for c in range(len(CHUNKS)):
                if root_step[c] + 1 == step:
                    finish(c)

        for q in range(4):
            queue = nc.sync if q % 2 else nc.scalar
            queue.dma_start(out_2[0, 4 * q : 4 * q + 4, :].bitcast(I32), y_plane[32 * q : 32 * q + 4, :].bitcast(I32))
